import numpy as np, ml_dtypes
CORES = [2,3,42,43,82,83,122,123]
N = 8
F = 256
def setup_inputs(rng):
    return {"x": rng.standard_normal((N, 128, N * F), dtype=np.float32).astype(ml_dtypes.bfloat16), "w": rng.standard_normal((N, 128, 128), dtype=np.float32).astype(ml_dtypes.bfloat16)}
def setup_inputs_big(rng):
    d = setup_inputs(rng)
    for k in ("x", "w"): d[k] = (d[k].astype(np.float32) * 1024.0).astype(d[k].dtype)
    return d
def setup_inputs_small(rng):
    d = setup_inputs(rng)
    for k in ("x", "w"): d[k] = (d[k].astype(np.float32) * (1 / 1024.0)).astype(d[k].dtype)
    return d
def setup_inputs_apart(rng):
    d = setup_inputs(rng)
    f = (10.0 ** rng.permutation(np.linspace(-1.5, 1.5, N))).astype(np.float32).reshape(N, 1, 1)
    for k in ("x", "w"): d[k] = (d[k].astype(np.float32) * f).astype(d[k].dtype)
    return d
def reference(x, w):
    X, W = x.astype(np.float64), w.astype(np.float64)
    s = X.sum(axis=0)
    o = np.concatenate([W[r].T @ s[:, F * r:F * r + F] for r in range(N)], axis=1).astype(ml_dtypes.bfloat16 if x.dtype != np.float64 else np.float64)
    return {"y": np.broadcast_to(o, (N,) + o.shape)}

@@ -1,0 +1,280 @@
+from concourse.bass import DstId, RemoteDMATransfer
+
+N = 8
+F = 256
+RPC = 2
+NCH = N // RPC
+CW = RPC * F
+
+SLOTS = ("r0", "h0", "r1", "h1")
+RS_HIER = True
+AG_FWD = True
+LAG = 2
+STORES_PER_CHUNK = 1
+
+NS = len(SLOTS)
+UW = CW // NS
+
+SCRATCH = {
+    "xs": ("sbuf", [128, N * F], "bfloat16"),
+    "ws": ("sbuf", [128, 128], "bfloat16"),
+    "wr": ("sbuf", [128, 128], "bfloat16"),
+    "lr0": ("sbuf", [128, N * F], "bfloat16"),
+    "lr1": ("sbuf", [128, N * F], "bfloat16"),
+    "lf": ("sbuf", [128, N * F], "bfloat16"),
+    "yb": ("sbuf", [128, N * F], "bfloat16"),
+    "ps": ("psum", [128, F], "float32"),
+}
+SEMAPHORES = (["wl", "wa", "mm", "cp", "sent", "sts", "stc"]
+              + ["ld%d" % d for d in range(NCH)]
+              + ["rw%d_%d" % (p, d) for p in range(RPC) for d in range(NCH)]
+              + ["fi%d" % s for s in range(N)]
+              + ["yy%d" % u for u in range(NCH * NS)]
+              + ["fw%d" % r for r in range(N)])
+
+
+def _bits(m):
+    return [i for i in range(m.bit_length()) if (m >> i) & 1]
+
+
+def _mask(engines):
+    m = 0
+    for i in engines:
+        m |= 1 << i
+    return m
+
+
+def _pow2(n):
+    e = 1
+    while e * 2 <= n:
+        e *= 2
+    return e
+
+
+def _layout(T, topo):
+    cores = list(T.cores)
+    chips = []
+    for c in cores:
+        if topo.chip(c) not in chips:
+            chips.append(topo.chip(c))
+    ranks = [[c for c in cores if topo.chip(c) == ch] for ch in chips]
+    every = range(topo.CHIPS * topo.CORES_PER_CHIP)
+    slot = []
+    for k, ch in enumerate(chips):
+        helpers = [c for c in every
+                   if topo.chip(c) == ch and c not in cores and topo.die(c) != topo.die(ranks[k][0])
+                   and all(topo.may_write(c, o) for o in cores)]
+        slot.append([(ranks[k] if s[0] == "r" else helpers)[int(s[1])] for s in SLOTS])
+    return ranks, slot
+
+
+def rank_program(g, core, T, topo):
+    ranks, slot = _layout(T, topo)
+    k = None
+    for kk in range(NCH):
+        if core in ranks[kk] or core in slot[kk]:
+            k = kk
+    if k is None:
+        return
+    pos = ranks[k].index(core) if core in ranks[k] else None
+    j = slot[k].index(core) if core in slot[k] else None
+    S = T.sem
+
+    def eng_sets(src):
+        kk = [q for q in range(NCH) if src in ranks[q] or src in slot[q]][0]
+        near = [c for c in ranks[kk] + slot[kk] if c != src][0]
+        far = slot[(kk + 1) % NCH][0]
+        full = _bits(topo.mask(src, near))
+        off = _bits(topo.mask(src, far))
+        hi = [e for e in full if e not in off]
+        return full, off, hi
+
+    full, off, hi = eng_sets(core)
+    pref = hi + off[::-1]
+
+    def raw_targets(kk, q):
+        return [(jj, slot[kk][jj]) for jj in range(NS) if slot[kk][jj] != q]
+
+    def e_raw(kk, q):
+        return _pow2(len(eng_sets(q)[0]) // len(raw_targets(kk, q)))
+
+    def e_flat(q):
+        return _pow2(len(eng_sets(q)[1]) // NS)
+
+    def e_off(q):
+        return len(eng_sets(q)[1])
+
+    def e_hi(q):
+        return len(eng_sets(q)[2])
+
+    def e_full(q):
+        return len(eng_sets(q)[0])
+
+    def ucols(d, jj):
+        return d * CW + jj * UW, d * CW + (jj + 1) * UW
+
+    def upos(jj):
+        return (jj * UW) // F
+
+    sent = [0]
+    waited = {}
+
+    def gw(name, cnt):
+        if waited.get(name, 0) < cnt:
+            g.wait_ge(S[name], cnt)
+            waited[name] = cnt
+
+    def tr(dsts, engines, sem, srcs, dst_ap, alu=0):
+        for d in dsts:
+            m = topo.mask(core, d)
+            for e in engines:
+                if not (m >> e) & 1 or not topo.may_write(core, d):
+                    raise ValueError("write %d -> %d not allowed" % (core, d))
+        ids = [DstId(rid=topo.addr(d)[0], pnc=topo.addr(d)[1]) for d in dsts]
+        sent[0] += len(engines)
+        return RemoteDMATransfer(dst_ids=ids, dma_engine_mask=_mask(engines), remote_sem=S[sem],
+                                 srcs=srcs, dsts=[dst_ap for d in dsts], alu_op=alu)
+
+    def call(trs):
+        g.remote_dma_fused(trs, local_sem=S.sent)
+
+    order = [(k + 1 + i) % NCH for i in range(NCH)]
+
+    if pos is not None:
+        g.scalar.dma_start(T.ws[:], T.w[:]).then_inc(S.wl, 16)
+        for i, d in enumerate(order):
+            q = g.sync if i % 2 == 0 else g.scalar
+            q.dma_start(T.xs[:, d * CW:(d + 1) * CW], T.x[:, d * CW:(d + 1) * CW]).then_inc(S["ld%d" % d], 16)
+        wt = [slot[k][jj] for jj in range(NS) if upos(jj) == pos and slot[k][jj] != core]
+        if wt:
+            gw("wl", 16)
+            call([tr(wt, full, "wa", [T.ws[:]], T.wr[:])])
+
+    def gather(d):
+        gw("ld%d" % d, 16)
+        if RS_HIER or d == k:
+            tg = raw_targets(k, core)
+            e = e_raw(k, core)
+            trs = []
+            for i, (jj, t) in enumerate(tg):
+                a, b = ucols(d, jj)
+                trs.append(tr([t], pref[i * e:(i + 1) * e], "rw%d_%d" % (pos, d), [T.xs[:, a:b]],
+                              T["lr%d" % pos][:, a:b]))
+        else:
+            me = k * RPC + pos
+            e = e_flat(core)
+            trs = []
+            for jj in range(NS):
+                a, b = ucols(d, jj)
+                trs.append(tr([slot[d][jj]], off[jj * e:(jj + 1) * e], "fi%d" % me, [T.xs[:, a:b]],
+                              T.lf[:, me * UW:(me + 1) * UW]))
+        if trs:
+            call(trs)
+
+    def fold(d):
+        a, b = ucols(d, j)
+        srcs = []
+        for p, q in enumerate(ranks[k]):
+            if q == core:
+                gw("ld%d" % d, 16)
+                srcs.append(T.xs[:, a:b])
+            else:
+                gw("rw%d_%d" % (p, d), e_raw(k, q))
+                srcs.append(T["lr%d" % p][:, a:b])
+        call([tr([slot[d][j]], off, "fi%d" % k, srcs, T.lf[:, k * UW:(k + 1) * UW], alu=1)])
+
+    folds = order[:-1] if (RS_HIER and j is not None) else []
+    nf = 0
+    for i, d in enumerate(order):
+        if pos is not None:
+            gather(d)
+        if i - (LAG - 1) >= 0 and nf < len(folds):
+            fold(folds[nf])
+            nf += 1
+    while nf < len(folds):
+        fold(folds[nf])
+        nf += 1
+
+    if j is not None:
+        t = g.tensor
+        if ranks[k][upos(j)] == core:
+            t.wait_ge(S.wl, 16)
+            w_ap = T.ws[:]
+        else:
+            t.wait_ge(S.wa, e_full(ranks[k][upos(j)]))
+            w_ap = T.wr[:]
+        a, b = ucols(k, j)
+        parts = []
+        for p, q in enumerate(ranks[k]):
+            if q == core:
+                parts.append(("ld%d" % k, 16, T.xs[:, a:b]))
+            else:
+                parts.append(("rw%d_%d" % (p, k), e_raw(k, q), T["lr%d" % p][:, a:b]))
+        for i in range(1, NCH):
+            s = (k - i) % NCH
+            if RS_HIER:
+                parts.append(("fi%d" % s, e_off(slot[s][j]), T.lf[:, s * UW:(s + 1) * UW]))
+            else:
+                for p, q in enumerate(ranks[s]):
+                    r = s * RPC + p
+                    parts.append(("fi%d" % r, e_flat(q), T.lf[:, r * UW:(r + 1) * UW]))
+        for i, (name, cnt, ap) in enumerate(parts):
+            t.wait_ge(S[name], cnt)
+            mm = t.matmul(T.ps[:, 0:UW], w_ap, ap, start=(i == 0), stop=(i == len(parts) - 1))
+        mm.then_inc(S.mm, 1)
+        g.vector.wait_ge(S.mm, 1)
+        g.vector.tensor_copy(T.yb[:, a:b], T.ps[:, 0:UW]).then_inc(S.cp, 1)
+
+        gw("cp", 1)
+        far = []
+        for i in range(1, NCH):
+            d = (k + i) % NCH
+            far += [ranks[d][upos(j)]] if AG_FWD else ranks[d]
+        call([tr(far, off, "yy%d" % (k * NS + j), [T.yb[:, a:b]], T.yb[:, a:b])])
+        near = [q for q in ranks[k] if q != core]
+        if near:
+            call([tr(near, hi, "yy%d" % (k * NS + j), [T.yb[:, a:b]], T.yb[:, a:b])])
+
+    if pos is not None:
+        if AG_FWD:
+            for i in range(1, NCH):
+                d = (k - i) % NCH
+                for jj in range(NS):
+                    if upos(jj) == pos:
+                        gw("yy%d" % (d * NS + jj), e_off(slot[d][jj]))
+                r = d * RPC + pos
+                call([tr([q for q in ranks[k] if q != core], full, "fw%d" % r, [T.yb[:, r * F:(r + 1) * F]],
+                         T.yb[:, r * F:(r + 1) * F])])
+
+        nst = {"sts": 0, "stc": 0}
+        idx = 0
+        per = NS // STORES_PER_CHUNK
+        for i in range(NCH):
+            d = (k - i) % NCH
+            for h in range(STORES_PER_CHUNK):
+                q, sem = (g.sync, "sts") if idx % 2 == 0 else (g.scalar, "stc")
+                idx += 1
+                needs = []
+                for jj in range(h * per, (h + 1) * per):
+                    wk = slot[d][jj]
+                    if wk == core:
+                        nd = ("cp", 1)
+                    elif d == k:
+                        nd = ("yy%d" % (d * NS + jj), e_hi(wk))
+                    elif not AG_FWD or upos(jj) == pos:
+                        nd = ("yy%d" % (d * NS + jj), e_off(wk))
+                    else:
+                        nd = ("fw%d" % (d * RPC + upos(jj)), e_full(ranks[k][upos(jj)]))
+                    if nd not in needs:
+                        needs.append(nd)
+                for name, cnt in needs:
+                    q.wait_ge(S[name], cnt)
+                a = d * CW + h * per * UW
+                b = a + per * UW
+                q.dma_start(T.y[:, a:b], T.yb[:, a:b]).then_inc(S[sem], 16)
+                nst[sem] += 16
+        g.sync.wait_ge(S.sts, nst["sts"])
+        g.scalar.wait_ge(S.stc, nst["stc"])
+
+    if sent[0]:
+        g.wait_ge(S.sent, sent[0])

@@ -7,13 +7,9 @@ NCH = N // RPC
 CW = RPC * F
 
 SLOTS = ("r0", "h0", "r1", "h1")
-RS_HIER = True
-AG_FWD = True
-LAG = 2
-STORES_PER_CHUNK = 1
-
 NS = len(SLOTS)
 UW = CW // NS
+DIRECT = 1
 
 SCRATCH = {
     "xs": ("sbuf", [128, N * F], "bfloat16"),
@@ -21,14 +17,14 @@ SCRATCH = {
     "wr": ("sbuf", [128, 128], "bfloat16"),
     "lr0": ("sbuf", [128, N * F], "bfloat16"),
     "lr1": ("sbuf", [128, N * F], "bfloat16"),
-    "lf": ("sbuf", [128, N * F], "bfloat16"),
+    "lf": ("sbuf", [128, NCH * UW], "bfloat16"),
     "yb": ("sbuf", [128, N * F], "bfloat16"),
     "ps": ("psum", [128, F], "float32"),
 }
 SEMAPHORES = (["wl", "wa", "mm", "cp", "sent", "sts", "stc"]
               + ["ld%d" % d for d in range(NCH)]
               + ["rw%d_%d" % (p, d) for p in range(RPC) for d in range(NCH)]
-              + ["fi%d" % s for s in range(N)]
+              + ["fi%d" % s for s in range(NCH)]
               + ["yy%d" % u for u in range(NCH * NS)]
               + ["fw%d" % r for r in range(N)])
 
@@ -77,7 +73,7 @@ def rank_program(g, core, T, topo):
     if k is None:
         return
     pos = ranks[k].index(core) if core in ranks[k] else None
-    j = slot[k].index(core) if core in slot[k] else None
+    j = slot[k].index(core)
     S = T.sem
 
     def eng_sets(src):
@@ -90,16 +86,6 @@ def rank_program(g, core, T, topo):
         return full, off, hi
 
     full, off, hi = eng_sets(core)
-    pref = hi + off[::-1]
-
-    def raw_targets(kk, q):
-        return [(jj, slot[kk][jj]) for jj in range(NS) if slot[kk][jj] != q]
-
-    def e_raw(kk, q):
-        return _pow2(len(eng_sets(q)[0]) // len(raw_targets(kk, q)))
-
-    def e_flat(q):
-        return _pow2(len(eng_sets(q)[1]) // NS)
 
     def e_off(q):
         return len(eng_sets(q)[1])
@@ -110,11 +96,33 @@ def rank_program(g, core, T, topo):
     def e_full(q):
         return len(eng_sets(q)[0])
 
+    def targets(kk, q, same=None):
+        return [(jj, slot[kk][jj]) for jj in range(NS) if slot[kk][jj] != q
+                and (same is None or (topo.die(slot[kk][jj]) == topo.die(q)) == same)]
+
     def ucols(d, jj):
         return d * CW + jj * UW, d * CW + (jj + 1) * UW
 
     def upos(jj):
         return (jj * UW) // F
+
+    def w_targets(kk, q):
+        return [slot[kk][jj] for jj in range(NS) if ranks[kk][upos(jj)] == q and slot[kk][jj] != q]
+
+    def e_raw(kk, q, t, d):
+        if d == kk:
+            return _pow2(e_full(q) // (len(targets(kk, q)) + 1))
+        if topo.die(t) == topo.die(q):
+            return _pow2(e_full(q) // ((NCH - 1) * len(targets(kk, q, True))))
+        return _pow2(e_full(q) // len(targets(kk, q, False)))
+
+    def e_w(kk, q):
+        return e_raw(kk, q, None, kk)
+
+    def e_fold(c, i):
+        if i > 1 and any(c in r for r in ranks):
+            return e_off(c) // (NCH - 2)
+        return e_off(c)
 
     sent = [0]
     waited = {}
@@ -145,134 +153,131 @@ def rank_program(g, core, T, topo):
         for i, d in enumerate(order):
             q = g.sync if i % 2 == 0 else g.scalar
             q.dma_start(T.xs[:, d * CW:(d + 1) * CW], T.x[:, d * CW:(d + 1) * CW]).then_inc(S["ld%d" % d], 16)
-        wt = [slot[k][jj] for jj in range(NS) if upos(jj) == pos and slot[k][jj] != core]
-        if wt:
+
+    def raw(lst, with_w=False):
+        trs = []
+        n = 0
+        for d, jj, t in lst:
+            gw("ld%d" % d, 16)
+            e = e_raw(k, core, t, d)
+            a, b = ucols(d, jj)
+            trs.append(tr([t], full[n:n + e], "rw%d_%d" % (pos, d), [T.xs[:, a:b]], T["lr%d" % pos][:, a:b]))
+            n += e
+        if with_w:
             gw("wl", 16)
-            call([tr(wt, full, "wa", [T.ws[:]], T.wr[:])])
+            e = e_w(k, core)
+            trs.append(tr(w_targets(k, core), full[n:n + e], "wa", [T.ws[:]], T.wr[:]))
+        call(trs)
 
-    def gather(d):
-        gw("ld%d" % d, 16)
-        if RS_HIER or d == k:
-            tg = raw_targets(k, core)
-            e = e_raw(k, core)
-            trs = []
-            for i, (jj, t) in enumerate(tg):
-                a, b = ucols(d, jj)
-                trs.append(tr([t], pref[i * e:(i + 1) * e], "rw%d_%d" % (pos, d), [T.xs[:, a:b]],
-                              T["lr%d" % pos][:, a:b]))
-        else:
-            me = k * RPC + pos
-            e = e_flat(core)
-            trs = []
-            for jj in range(NS):
-                a, b = ucols(d, jj)
-                trs.append(tr([slot[d][jj]], off[jj * e:(jj + 1) * e], "fi%d" % me, [T.xs[:, a:b]],
-                              T.lf[:, me * UW:(me + 1) * UW]))
-        if trs:
-            call(trs)
-
-    def fold(d):
-        a, b = ucols(d, j)
-        srcs = []
-        for p, q in enumerate(ranks[k]):
-            if q == core:
-                gw("ld%d" % d, 16)
-                srcs.append(T.xs[:, a:b])
-            else:
-                gw("rw%d_%d" % (p, d), e_raw(k, q))
-                srcs.append(T["lr%d" % p][:, a:b])
-        call([tr([slot[d][j]], off, "fi%d" % k, srcs, T.lf[:, k * UW:(k + 1) * UW], alu=1)])
-
-    folds = order[:-1] if (RS_HIER and j is not None) else []
-    nf = 0
-    for i, d in enumerate(order):
-        if pos is not None:
-            gather(d)
-        if i - (LAG - 1) >= 0 and nf < len(folds):
-            fold(folds[nf])
-            nf += 1
-    while nf < len(folds):
-        fold(folds[nf])
-        nf += 1
-
-    if j is not None:
-        t = g.tensor
-        if ranks[k][upos(j)] == core:
-            t.wait_ge(S.wl, 16)
-            w_ap = T.ws[:]
-        else:
-            t.wait_ge(S.wa, e_full(ranks[k][upos(j)]))
-            w_ap = T.wr[:]
-        a, b = ucols(k, j)
-        parts = []
-        for p, q in enumerate(ranks[k]):
-            if q == core:
-                parts.append(("ld%d" % k, 16, T.xs[:, a:b]))
-            else:
-                parts.append(("rw%d_%d" % (p, k), e_raw(k, q), T["lr%d" % p][:, a:b]))
-        for i in range(1, NCH):
-            s = (k - i) % NCH
-            if RS_HIER:
-                parts.append(("fi%d" % s, e_off(slot[s][j]), T.lf[:, s * UW:(s + 1) * UW]))
-            else:
-                for p, q in enumerate(ranks[s]):
-                    r = s * RPC + p
-                    parts.append(("fi%d" % r, e_flat(q), T.lf[:, r * UW:(r + 1) * UW]))
-        for i, (name, cnt, ap) in enumerate(parts):
-            t.wait_ge(S[name], cnt)
-            mm = t.matmul(T.ps[:, 0:UW], w_ap, ap, start=(i == 0), stop=(i == len(parts) - 1))
-        mm.then_inc(S.mm, 1)
-        g.vector.wait_ge(S.mm, 1)
-        g.vector.tensor_copy(T.yb[:, a:b], T.ps[:, 0:UW]).then_inc(S.cp, 1)
-
-        gw("cp", 1)
-        far = []
-        for i in range(1, NCH):
-            d = (k + i) % NCH
-            far += [ranks[d][upos(j)]] if AG_FWD else ranks[d]
-        call([tr(far, off, "yy%d" % (k * NS + j), [T.yb[:, a:b]], T.yb[:, a:b])])
-        near = [q for q in ranks[k] if q != core]
-        if near:
-            call([tr(near, hi, "yy%d" % (k * NS + j), [T.yb[:, a:b]], T.yb[:, a:b])])
+    def fold(idx):
+        trs = []
+        n = 0
+        for i in idx:
+            d = order[i - 1]
+            a, b = ucols(d, j)
+            srcs = []
+            for p, q in enumerate(ranks[k]):
+                if q == core:
+                    gw("ld%d" % d, 16)
+                    srcs.append(T.xs[:, a:b])
+                else:
+                    gw("rw%d_%d" % (p, d), e_raw(k, q, core, d))
+                    srcs.append(T["lr%d" % p][:, a:b])
+            e = e_fold(core, i)
+            trs.append(tr([slot[d][j]], off[n:n + e], "fi%d" % k, srcs, T.lf[:, k * UW:(k + 1) * UW], alu=1))
+            n += e
+        call(trs)
 
     if pos is not None:
-        if AG_FWD:
-            for i in range(1, NCH):
-                d = (k - i) % NCH
-                for jj in range(NS):
-                    if upos(jj) == pos:
-                        gw("yy%d" % (d * NS + jj), e_off(slot[d][jj]))
-                r = d * RPC + pos
-                call([tr([q for q in ranks[k] if q != core], full, "fw%d" % r, [T.yb[:, r * F:(r + 1) * F]],
-                         T.yb[:, r * F:(r + 1) * F])])
+        for d in order[:-1]:
+            raw([(d, jj, t) for jj, t in targets(k, core, False)])
+        raw([(d, jj, t) for d in order[:-1] for jj, t in targets(k, core, True)])
+        raw([(k, jj, t) for jj, t in targets(k, core)], with_w=True)
+        fold([1])
+        fold(list(range(2, NCH)))
+    else:
+        for i in range(1, NCH):
+            fold([i])
+
+    t = g.tensor
+    owner = ranks[k][upos(j)]
+    if owner == core:
+        t.wait_ge(S.wl, 16)
+        w_ap = T.ws[:]
+    else:
+        t.wait_ge(S.wa, e_w(k, owner))
+        w_ap = T.wr[:]
+    a, b = ucols(k, j)
+    parts = []
+    for p, q in enumerate(ranks[k]):
+        if q == core:
+            parts.append(("ld%d" % k, 16, T.xs[:, a:b]))
+        else:
+            parts.append(("rw%d_%d" % (p, k), e_raw(k, q, core, k), T["lr%d" % p][:, a:b]))
+    for i in range(1, NCH):
+        s = (k - i) % NCH
+        parts.append(("fi%d" % s, e_fold(slot[s][j], i), T.lf[:, s * UW:(s + 1) * UW]))
+    for i, (name, cnt, ap) in enumerate(parts):
+        t.wait_ge(S[name], cnt)
+        mm = t.matmul(T.ps[:, 0:UW], w_ap, ap, start=(i == 0), stop=(i == len(parts) - 1))
+    mm.then_inc(S.mm, 1)
+    g.vector.wait_ge(S.mm, 1)
+    g.vector.tensor_copy(T.yb[:, a:b], T.ps[:, 0:UW]).then_inc(S.cp, 1)
+
+    def direct(i):
+        return i >= NCH - DIRECT
+
+    gw("cp", 1)
+    far = []
+    for i in range(1, NCH):
+        rk = ranks[(k + i) % NCH]
+        far += [rk[upos(j)]] + ([q for q in rk if q != rk[upos(j)]] if direct(i) else [])
+    call([tr(far, off, "yy%d" % (k * NS + j), [T.yb[:, a:b]], T.yb[:, a:b])])
+    near = [q for q in ranks[k] if q != core]
+    call([tr(near, hi, "yy%d" % (k * NS + j), [T.yb[:, a:b]], T.yb[:, a:b])])
+
+    if pos is not None:
+        for i in range(1, NCH):
+            if direct(i):
+                continue
+            d = (k - i) % NCH
+            for jj in range(NS):
+                if upos(jj) == pos:
+                    gw("yy%d" % (d * NS + jj), e_off(slot[d][jj]))
+            r = d * RPC + pos
+            call([tr([q for q in ranks[k] if q != core], full, "fw%d" % r, [T.yb[:, r * F:(r + 1) * F]],
+                     T.yb[:, r * F:(r + 1) * F])])
 
         nst = {"sts": 0, "stc": 0}
-        idx = 0
-        per = NS // STORES_PER_CHUNK
-        for i in range(NCH):
+
+        def store(q, sem, i, js):
             d = (k - i) % NCH
-            for h in range(STORES_PER_CHUNK):
-                q, sem = (g.sync, "sts") if idx % 2 == 0 else (g.scalar, "stc")
-                idx += 1
-                needs = []
-                for jj in range(h * per, (h + 1) * per):
-                    wk = slot[d][jj]
-                    if wk == core:
-                        nd = ("cp", 1)
-                    elif d == k:
-                        nd = ("yy%d" % (d * NS + jj), e_hi(wk))
-                    elif not AG_FWD or upos(jj) == pos:
-                        nd = ("yy%d" % (d * NS + jj), e_off(wk))
-                    else:
-                        nd = ("fw%d" % (d * RPC + upos(jj)), e_full(ranks[k][upos(jj)]))
-                    if nd not in needs:
-                        needs.append(nd)
-                for name, cnt in needs:
-                    q.wait_ge(S[name], cnt)
-                a = d * CW + h * per * UW
-                b = a + per * UW
-                q.dma_start(T.y[:, a:b], T.yb[:, a:b]).then_inc(S[sem], 16)
-                nst[sem] += 16
+            needs = []
+            for jj in js:
+                wk = slot[d][jj]
+                if wk == core:
+                    nd = ("cp", 1)
+                elif d == k:
+                    nd = ("yy%d" % (d * NS + jj), e_hi(wk))
+                elif upos(jj) == pos or direct(i):
+                    nd = ("yy%d" % (d * NS + jj), e_off(wk))
+                else:
+                    nd = ("fw%d" % (d * RPC + upos(jj)), e_full(ranks[k][upos(jj)]))
+                if nd not in needs:
+                    needs.append(nd)
+            for name, cnt in needs:
+                q.wait_ge(S[name], cnt)
+            c0, c1 = ucols(d, js[0])[0], ucols(d, js[-1])[1]
+            q.dma_start(T.y[:, c0:c1], T.yb[:, c0:c1]).then_inc(S[sem], 16)
+            nst[sem] += 16
+
+        for i in range(NCH):
+            q, sem = (g.sync, "sts") if i % 2 == 0 else (g.scalar, "stc")
+            if direct(i):
+                store(q, sem, i, [jj for jj in range(NS) if upos(jj) == pos])
+                store(q, sem, i, [jj for jj in range(NS) if upos(jj) != pos])
+            else:
+                store(q, sem, i, list(range(NS)))
         g.sync.wait_ge(S.sts, nst["sts"])
         g.scalar.wait_ge(S.stc, nst["stc"])
 

from concourse.bass import DstId, RemoteDMATransfer

N = 8
F = 256
RPC = 2
NCH = N // RPC
CW = RPC * F

SLOTS = ("r0", "h0", "r1", "h1")
NS = len(SLOTS)
UW = CW // NS
DIRECT = 1

SCRATCH = {
    "xs": ("sbuf", [128, N * F], "bfloat16"),
    "ws": ("sbuf", [128, 128], "bfloat16"),
    "wr": ("sbuf", [128, 128], "bfloat16"),
    "lr0": ("sbuf", [128, N * F], "bfloat16"),
    "lr1": ("sbuf", [128, N * F], "bfloat16"),
    "lf": ("sbuf", [128, NCH * UW], "bfloat16"),
    "yb": ("sbuf", [128, N * F], "bfloat16"),
    "ps": ("psum", [128, F], "float32"),
}
SEMAPHORES = (["wl", "wa", "mm", "cp", "sent", "sts", "stc"]
              + ["ld%d" % d for d in range(NCH)]
              + ["rw%d_%d" % (p, d) for p in range(RPC) for d in range(NCH)]
              + ["fi%d" % s for s in range(NCH)]
              + ["yy%d" % u for u in range(NCH * NS)]
              + ["fw%d" % r for r in range(N)])


def _bits(m):
    return [i for i in range(m.bit_length()) if (m >> i) & 1]


def _mask(engines):
    m = 0
    for i in engines:
        m |= 1 << i
    return m


def _pow2(n):
    e = 1
    while e * 2 <= n:
        e *= 2
    return e


def _layout(T, topo):
    cores = list(T.cores)
    chips = []
    for c in cores:
        if topo.chip(c) not in chips:
            chips.append(topo.chip(c))
    ranks = [[c for c in cores if topo.chip(c) == ch] for ch in chips]
    every = range(topo.CHIPS * topo.CORES_PER_CHIP)
    slot = []
    for k, ch in enumerate(chips):
        helpers = [c for c in every
                   if topo.chip(c) == ch and c not in cores and topo.die(c) != topo.die(ranks[k][0])
                   and all(topo.may_write(c, o) for o in cores)]
        slot.append([(ranks[k] if s[0] == "r" else helpers)[int(s[1])] for s in SLOTS])
    return ranks, slot


def rank_program(g, core, T, topo):
    ranks, slot = _layout(T, topo)
    k = None
    for kk in range(NCH):
        if core in ranks[kk] or core in slot[kk]:
            k = kk
    if k is None:
        return
    pos = ranks[k].index(core) if core in ranks[k] else None
    j = slot[k].index(core)
    S = T.sem

    def eng_sets(src):
        kk = [q for q in range(NCH) if src in ranks[q] or src in slot[q]][0]
        near = [c for c in ranks[kk] + slot[kk] if c != src][0]
        far = slot[(kk + 1) % NCH][0]
        full = _bits(topo.mask(src, near))
        off = _bits(topo.mask(src, far))
        hi = [e for e in full if e not in off]
        return full, off, hi

    full, off, hi = eng_sets(core)

    def e_off(q):
        return len(eng_sets(q)[1])

    def e_hi(q):
        return len(eng_sets(q)[2])

    def e_full(q):
        return len(eng_sets(q)[0])

    def targets(kk, q, same=None):
        return [(jj, slot[kk][jj]) for jj in range(NS) if slot[kk][jj] != q
                and (same is None or (topo.die(slot[kk][jj]) == topo.die(q)) == same)]

    def ucols(d, jj):
        return d * CW + jj * UW, d * CW + (jj + 1) * UW

    def upos(jj):
        return (jj * UW) // F

    def w_targets(kk, q):
        return [slot[kk][jj] for jj in range(NS) if ranks[kk][upos(jj)] == q and slot[kk][jj] != q]

    def e_raw(kk, q, t, d):
        if d == kk:
            return _pow2(e_full(q) // (len(targets(kk, q)) + 1))
        if topo.die(t) == topo.die(q):
            return _pow2(e_full(q) // ((NCH - 1) * len(targets(kk, q, True))))
        return _pow2(e_full(q) // len(targets(kk, q, False)))

    def e_w(kk, q):
        return e_raw(kk, q, None, kk)

    def e_fold(c, i):
        if i > 1 and any(c in r for r in ranks):
            return e_off(c) // (NCH - 2)
        return e_off(c)

    sent = [0]
    waited = {}

    def gw(name, cnt):
        if waited.get(name, 0) < cnt:
            g.wait_ge(S[name], cnt)
            waited[name] = cnt

    def tr(dsts, engines, sem, srcs, dst_ap, alu=0):
        for d in dsts:
            m = topo.mask(core, d)
            for e in engines:
                if not (m >> e) & 1 or not topo.may_write(core, d):
                    raise ValueError("write %d -> %d not allowed" % (core, d))
        ids = [DstId(rid=topo.addr(d)[0], pnc=topo.addr(d)[1]) for d in dsts]
        sent[0] += len(engines)
        return RemoteDMATransfer(dst_ids=ids, dma_engine_mask=_mask(engines), remote_sem=S[sem],
                                 srcs=srcs, dsts=[dst_ap for d in dsts], alu_op=alu)

    def call(trs):
        g.remote_dma_fused(trs, local_sem=S.sent)

    order = [(k + 1 + i) % NCH for i in range(NCH)]

    if pos is not None:
        g.scalar.dma_start(T.ws[:], T.w[:]).then_inc(S.wl, 16)
        for i, d in enumerate(order):
            q = g.sync if i % 2 == 0 else g.scalar
            q.dma_start(T.xs[:, d * CW:(d + 1) * CW], T.x[:, d * CW:(d + 1) * CW]).then_inc(S["ld%d" % d], 16)

    def raw(lst, with_w=False):
        trs = []
        n = 0
        for d, jj, t in lst:
            gw("ld%d" % d, 16)
            e = e_raw(k, core, t, d)
            a, b = ucols(d, jj)
            trs.append(tr([t], full[n:n + e], "rw%d_%d" % (pos, d), [T.xs[:, a:b]], T["lr%d" % pos][:, a:b]))
            n += e
        if with_w:
            gw("wl", 16)
            e = e_w(k, core)
            trs.append(tr(w_targets(k, core), full[n:n + e], "wa", [T.ws[:]], T.wr[:]))
        call(trs)

    def fold(idx):
        trs = []
        n = 0
        for i in idx:
            d = order[i - 1]
            a, b = ucols(d, j)
            srcs = []
            for p, q in enumerate(ranks[k]):
                if q == core:
                    gw("ld%d" % d, 16)
                    srcs.append(T.xs[:, a:b])
                else:
                    gw("rw%d_%d" % (p, d), e_raw(k, q, core, d))
                    srcs.append(T["lr%d" % p][:, a:b])
            e = e_fold(core, i)
            trs.append(tr([slot[d][j]], off[n:n + e], "fi%d" % k, srcs, T.lf[:, k * UW:(k + 1) * UW], alu=1))
            n += e
        call(trs)

    if pos is not None:
        for d in order[:-1]:
            raw([(d, jj, t) for jj, t in targets(k, core, False)])
        raw([(d, jj, t) for d in order[:-1] for jj, t in targets(k, core, True)])
        raw([(k, jj, t) for jj, t in targets(k, core)], with_w=True)
        fold([1])
        fold(list(range(2, NCH)))
    else:
        for i in range(1, NCH):
            fold([i])

    t = g.tensor
    owner = ranks[k][upos(j)]
    if owner == core:
        t.wait_ge(S.wl, 16)
        w_ap = T.ws[:]
    else:
        t.wait_ge(S.wa, e_w(k, owner))
        w_ap = T.wr[:]
    a, b = ucols(k, j)
    parts = []
    for p, q in enumerate(ranks[k]):
        if q == core:
            parts.append(("ld%d" % k, 16, T.xs[:, a:b]))
        else:
            parts.append(("rw%d_%d" % (p, k), e_raw(k, q, core, k), T["lr%d" % p][:, a:b]))
    for i in range(1, NCH):
        s = (k - i) % NCH
        parts.append(("fi%d" % s, e_fold(slot[s][j], i), T.lf[:, s * UW:(s + 1) * UW]))
    for i, (name, cnt, ap) in enumerate(parts):
        t.wait_ge(S[name], cnt)
        mm = t.matmul(T.ps[:, 0:UW], w_ap, ap, start=(i == 0), stop=(i == len(parts) - 1))
    mm.then_inc(S.mm, 1)
    g.vector.wait_ge(S.mm, 1)
    g.vector.tensor_copy(T.yb[:, a:b], T.ps[:, 0:UW]).then_inc(S.cp, 1)

    def direct(i):
        return i >= NCH - DIRECT

    gw("cp", 1)
    far = []
    for i in range(1, NCH):
        rk = ranks[(k + i) % NCH]
        far += [rk[upos(j)]] + ([q for q in rk if q != rk[upos(j)]] if direct(i) else [])
    call([tr(far, off, "yy%d" % (k * NS + j), [T.yb[:, a:b]], T.yb[:, a:b])])
    near = [q for q in ranks[k] if q != core]
    call([tr(near, hi, "yy%d" % (k * NS + j), [T.yb[:, a:b]], T.yb[:, a:b])])

    if pos is not None:
        for i in range(1, NCH):
            if direct(i):
                continue
            d = (k - i) % NCH
            for jj in range(NS):
                if upos(jj) == pos:
                    gw("yy%d" % (d * NS + jj), e_off(slot[d][jj]))
            r = d * RPC + pos
            call([tr([q for q in ranks[k] if q != core], full, "fw%d" % r, [T.yb[:, r * F:(r + 1) * F]],
                     T.yb[:, r * F:(r + 1) * F])])

        nst = {"sts": 0, "stc": 0}

        def store(q, sem, i, js):
            d = (k - i) % NCH
            needs = []
            for jj in js:
                wk = slot[d][jj]
                if wk == core:
                    nd = ("cp", 1)
                elif d == k:
                    nd = ("yy%d" % (d * NS + jj), e_hi(wk))
                elif upos(jj) == pos or direct(i):
                    nd = ("yy%d" % (d * NS + jj), e_off(wk))
                else:
                    nd = ("fw%d" % (d * RPC + upos(jj)), e_full(ranks[k][upos(jj)]))
                if nd not in needs:
                    needs.append(nd)
            for name, cnt in needs:
                q.wait_ge(S[name], cnt)
            c0, c1 = ucols(d, js[0])[0], ucols(d, js[-1])[1]
            q.dma_start(T.y[:, c0:c1], T.yb[:, c0:c1]).then_inc(S[sem], 16)
            nst[sem] += 16

        for i in range(NCH):
            q, sem = (g.sync, "sts") if i % 2 == 0 else (g.scalar, "stc")
            if direct(i):
                store(q, sem, i, [jj for jj in range(NS) if upos(jj) == pos])
                store(q, sem, i, [jj for jj in range(NS) if upos(jj) != pos])
            else:
                store(q, sem, i, list(range(NS)))
        g.sync.wait_ge(S.sts, nst["sts"])
        g.scalar.wait_ge(S.stc, nst["stc"])

    if sent[0]:
        g.wait_ge(S.sent, sent[0])
